import numpy as np
import ml_dtypes


def mxq(x, axis, fmt="e4m3"):
    dtype, down = {"e4m3": (ml_dtypes.float8_e4m3fn, 7), "e5m2": (ml_dtypes.float8_e5m2, 14)}[fmt]
    v = np.moveaxis(np.asarray(x, np.float32).astype(ml_dtypes.bfloat16).astype(np.float64), axis, -1)
    blocks = v.reshape(v.shape[:-1] + (-1, 32))
    amax = np.abs(blocks).max(-1, keepdims=True)
    byte = np.maximum(np.where(amax > 0, np.frexp(amax)[1] - 1 + 127, 0) - down, 1)
    scale = np.exp2(byte - 127.0)
    codes = (blocks / scale).astype(np.float32).astype(dtype).astype(np.float64)
    return np.moveaxis((codes * scale).reshape(v.shape), -1, axis)


WIDE = False


def mx_kscale(k):
    if not WIDE:
        return np.ones(k)
    levels = np.array([10, -10, 5, -5, 0])
    if k % 512:
        return np.exp2(np.random.permutation(np.resize(levels, k // 32))).repeat(32)
    a = np.empty((k // 512, 16))
    for p in range(k // 512):
        a[p, :8] = np.random.permutation(np.resize(levels, 8))
        for g in range(8):
            far = levels[np.abs(levels - a[p, g]) >= 10]
            a[p, g + 8] = far[np.random.randint(len(far))]
    return np.exp2(a.ravel()).repeat(32)


BF16 = ml_dtypes.bfloat16


def bf(x):
    return np.asarray(x, np.float32).astype(BF16)


def f64(x):
    return np.asarray(x).astype(np.float64)

def planes(Y):
    n, m = Y.shape
    b = f64(bf(Y)).reshape(n // 32, 32, m)
    amax = np.abs(b).max(1)
    byte = np.clip(np.where(amax > 0, np.frexp(amax)[1] - 1 + 127 - 7, 1), 1, 254)
    codes = (b * np.exp2(127.0 - byte)[:, None, :]).reshape(n, m).astype(np.float32).astype(ml_dtypes.float8_e4m3fn).view(np.uint8)
    words = codes.reshape(n // 512, 128, 4, m).transpose(0, 1, 3, 2)
    return np.ascontiguousarray(words), np.ascontiguousarray(byte.astype(np.uint8).reshape(n // 512, 16, m))


H, L, D, F = 4, 1024, 512, 1024


def setup_inputs():
    s = mx_kscale(D)
    length = np.random.uniform(0.5, 1.0, (H, L, 1))
    k = length * np.random.randn(H, L, D) / np.sqrt(D)
    half_norm = 0.5 * np.sum(k * k, axis=2)
    omega = np.random.randn(D, F)
    key_gate = np.exp(0.8 * np.random.randn(H, L))
    return {
        "keys": bf(k * s),
        "omega": bf(omega / s[:, None]),
        "half_norm": bf(half_norm),
        "key_gate": bf(key_gate),
    }

def reference(keys, omega, half_norm, key_gate):
    k = mxq(f64(keys).reshape(H * L, D), 1, "e4m3")
    w = mxq(f64(omega), 0, "e4m3")
    proj = (k @ w).reshape(H, L, F)
    feat = np.exp(proj - f64(half_norm)[:, :, None])
    y = feat * f64(key_gate)[:, :, None]
    Y = y.transpose(1, 0, 2).reshape(L, H * F)
    words, scales = planes(Y)
    return y, words, scales

@@ -1,0 +1,300 @@
+from contextlib import ExitStack
+
+import concourse.mybir as mybir
+from concourse.masks import make_identity
+
+H, L, D, F = 4, 1024, 512, 1024
+FLOPS = 2 * H * L * D * F
+
+F32 = mybir.dt.float32
+BF16 = mybir.dt.bfloat16
+I32 = mybir.dt.int32
+U32 = mybir.dt.uint32
+U8 = mybir.dt.uint8
+FP8X4 = mybir.dt.float8_e4m3fn_x4
+ACT = mybir.ActivationFunctionType
+ALU = mybir.AluOpType
+
+P = 128
+PACK = 4
+GROUP = P * PACK
+GROUPS = L // GROUP
+HALF = 512
+HALVES = F // HALF
+RUN = 4
+UNITS = [(g, h) for g in range(GROUPS) for h in range(H)]
+LAST = len(UNITS) - 1
+
+
+def tile_gated_positive_key_features_g2_kernel(tc, keys, omega, half_norm, key_gate, out_0, out_1, out_2):
+    nc = tc.nc
+    words_hbm = out_1.rearrange("g p m t -> g p (m t)").bitcast(I32)
+    scales_hbm = out_2.bitcast(I32)
+
+    with ExitStack() as ctx:
+        keep = ctx.enter_context(tc.tile_pool(name="keep", bufs=1))
+        work = ctx.enter_context(tc.tile_pool(name="work", bufs=2))
+        proj_banks = ctx.enter_context(tc.psum_pool(name="proj_banks", bufs=6))
+        turn_banks = ctx.enter_context(tc.psum_pool(name="turn_banks", bufs=2))
+        ctx.enter_context(tc.manual_schedule())
+
+        identity = keep.tile([P, P], F32, name="identity")
+        make_identity(nc, identity[:])
+        per_key = keep.tile([P, GROUP], BF16, name="per_key")
+        nc.vector.memset(per_key[:], 0.0)
+
+        omega_raw = {}
+        keys_raw = {}
+
+        def load_omega(half):
+            omega_raw[half] = keep.tile([P, PACK, HALF], BF16, name="omega_raw%d" % half)
+            cols = omega[:, half * HALF : (half + 1) * HALF]
+            nc.sync.dma_start(out=omega_raw[half][:], in_=cols.rearrange("(p j) f -> p j f", j=PACK))
+
+        def load_keys(u, t0, t1):
+            g, h = UNITS[u]
+            raw = keep.tile([P, t1 - t0, D], BF16, name="keys_raw%d_%d" % (u, t0))
+            rows = keys[h, g * GROUP : (g + 1) * GROUP, :].rearrange("(p t) d -> p t d", t=PACK)
+            nc.sync.dma_start(out=raw[:], in_=rows[:, t0:t1, :])
+            for t in range(t0, t1):
+                keys_raw[u, t] = raw[:, t - t0, :]
+
+        rows_per_input = H * GROUPS
+        load_omega(0)
+        nc.sync.dma_start(
+            out=per_key[0:rows_per_input, :], in_=half_norm.rearrange("h (g l) -> (h g) l", g=GROUPS)
+        )
+        nc.sync.dma_start(
+            out=per_key[rows_per_input : 2 * rows_per_input, :],
+            in_=key_gate.rearrange("h (g l) -> (h g) l", g=GROUPS),
+        )
+        load_keys(0, 0, 2)
+        load_keys(0, 2, 4)
+        load_omega(1)
+        for u in range(1, len(UNITS)):
+            load_keys(u, 0, PACK)
+
+        per_key_turned = proj_banks.tile([P, 2, P], F32, name="per_key_turned", tag="proj")
+        per_key_words = per_key[:].bitcast(F32)
+        for w in range(2):
+            nc.tensor.transpose(per_key_turned[:, w, :], per_key_words[:, w : GROUP // 2 : 2], identity[:])
+        turned_values = per_key_turned[:].bitcast(BF16)
+        neg_norm = keep.tile([P, 2, 2 * rows_per_input], F32, name="neg_norm")
+        gate = keep.tile([P, 2, 2 * rows_per_input], F32, name="gate")
+        nc.scalar.activation(neg_norm[:], turned_values[:, :, 0 : 2 * rows_per_input], ACT.Copy, scale=-1.0)
+        nc.scalar.copy(gate[:], turned_values[:, :, 2 * rows_per_input : 4 * rows_per_input])
+
+        def per_key_column(table, u, t):
+            g, h = UNITS[u]
+            col = 2 * (h * GROUPS + g) + t % 2
+            return table[:, t // 2, col : col + 1]
+
+        def interleave(dst, src):
+            nc.vector.tensor_copy(
+                out=dst.rearrange("p (c i) t -> p c t i", i=RUN),
+                in_=src.rearrange("p t (c i) -> p c t i", i=RUN),
+            )
+
+        omega_grouped = {}
+        omega_codes = {}
+        omega_scales = {}
+
+        def interleave_omega(half):
+            omega_grouped[half] = keep.tile([P, HALF, PACK], BF16, name="omega_grouped%d" % half, align_bytes=64)
+            interleave(omega_grouped[half][:], omega_raw[half][:])
+
+        def quantize_omega(half):
+            omega_codes[half] = keep.tile([P, HALF], U32, name="omega_codes%d" % half, align_bytes=64)
+            omega_scales[half] = keep.tile([P, HALF], U8, name="omega_scales%d" % half, align_bytes=64)
+            nc.vector.quantize_mx(
+                out=omega_codes[half][:].bitcast(FP8X4),
+                scales=omega_scales[half][:],
+                in_=omega_grouped[half][:].rearrange("p f j -> p (f j)"),
+            )
+
+        keys_turned = {}
+        keys_grouped = {}
+        key_codes = {}
+        key_scales = {}
+
+        def turn_keys(u, pair):
+            bank = turn_banks.tile([P, 2, 2, P], F32, name="keys_turned", tag="turn")
+            keys_turned[u, pair] = bank
+            for s in range(2):
+                words = keys_raw[u, 2 * pair + s].bitcast(F32)
+                for w in range(2):
+                    nc.tensor.transpose(bank[:, s, w, :], words[:, w : D // 2 : 2], identity[:])
+
+        def new_keys_grouped(u, pair0, pairs):
+            grouped = work.tile([P, pairs * 2 * P * PACK], BF16, name="keys_grouped", align_bytes=64)
+            for k in range(pairs):
+                keys_grouped[u, pair0 + k] = (grouped, k)
+
+        def evict_keys(u, pair):
+            grouped, k = keys_grouped[u, pair]
+            width = 2 * P * PACK
+            dst = grouped[:, k * width : (k + 1) * width].bitcast(F32)
+            nc.scalar.copy(
+                dst.rearrange("p (s m w) -> p s m w", s=2, w=2),
+                keys_turned[u, pair][:].rearrange("p s w m -> p s m w"),
+            )
+
+        def quantize_keys(u, pair0, pairs):
+            if pair0 == 0:
+                key_codes[u] = work.tile([P, PACK * P], U32, name="key_codes", bufs=3, align_bytes=64)
+                key_scales[u] = work.tile([P, PACK * P], U8, name="key_scales", bufs=3, align_bytes=64)
+            cols = slice(pair0 * 2 * P, (pair0 + pairs) * 2 * P)
+            nc.vector.quantize_mx(
+                out=key_codes[u][:, cols].bitcast(FP8X4),
+                scales=key_scales[u][:, cols],
+                in_=keys_grouped[u, pair0][0][:],
+            )
+
+        y = {}
+        y_grouped = {}
+        y_words = {}
+        y_scales = {}
+
+        def project_and_exp(u, t, half):
+            bank = proj_banks.tile([P, HALF], F32, name="proj", tag="proj")
+            cols = slice(t * P, (t + 1) * P)
+            nc.tensor.matmul_mx(
+                out=bank[:],
+                lhsT=key_codes[u][:, cols].bitcast(FP8X4),
+                lhsT_scale=key_scales[u][:, cols],
+                rhs=omega_codes[half][:].bitcast(FP8X4),
+                rhs_scale=omega_scales[half][:],
+                start=True,
+                stop=True,
+            )
+            nc.scalar.activation(
+                y[u][:, t, half * HALF : (half + 1) * HALF], bank[:], ACT.Exp, bias=per_key_column(neg_norm, u, t)
+            )
+
+        def gate_on_vector(u, t, half0, half1):
+            part = y[u][:, t, half0 * HALF : half1 * HALF]
+            nc.vector.tensor_scalar(part, part, per_key_column(gate, u, t), None, ALU.mult)
+
+        def gate_on_scalar(u, t, half):
+            part = y[u][:, t, half * HALF : (half + 1) * HALF]
+            nc.scalar.activation(part, part, ACT.Copy, scale=per_key_column(gate, u, t))
+
+        def store_y(u, t0, t1, half0, half1):
+            g, h = UNITS[u]
+            rows = out_0[h, g * GROUP : (g + 1) * GROUP, :].rearrange("(p t) f -> p t f", t=PACK)
+            cols = slice(half0 * HALF, half1 * HALF)
+            nc.sync.dma_start(out=rows[:, t0:t1, cols], in_=y[u][:, t0:t1, cols])
+
+        def interleave_y(u, half):
+            y_grouped[u, half] = work.tile([P, HALF, PACK], BF16, name="y_grouped", bufs=3, align_bytes=64)
+            interleave(y_grouped[u, half][:], y[u][:, :, half * HALF : (half + 1) * HALF])
+
+        def store_words(g, m0, m1):
+            nc.sync.dma_start(out=words_hbm[g, :, m0:m1], in_=y_words[g][:, m0:m1].bitcast(I32))
+
+        def store_scales(g):
+            width = F // 4
+            for q in range(4):
+                rows = scales_hbm[g, 4 * q : 4 * q + 4, :].rearrange("r (h m) -> h r m", m=width)
+                nc.sync.dma_start(out=rows, in_=y_scales[g][32 * q : 32 * q + 4 * H, :].bitcast(I32))
+
+        def quantize_y(u, half):
+            g, h = UNITS[u]
+            if h == 0 and half == 0:
+                y_words[g] = work.tile([P, H * F], U32, name="y_words", align_bytes=64)
+                y_scales[g] = work.tile([P, F], U8, name="y_scales", align_bytes=64)
+            m0 = h * F + half * HALF
+            nc.vector.quantize_mx(
+                out=y_words[g][:, m0 : m0 + HALF].bitcast(FP8X4),
+                scales=y_scales[g][4 * h : P, half * HALF : (half + 1) * HALF],
+                in_=y_grouped[u, half][:].rearrange("p f t -> p (f t)"),
+            )
+            if u == LAST:
+                store_words(g, m0, m0 + HALF)
+            elif half == 1 and u == LAST - 1:
+                store_words(g, h * F, (h + 1) * F)
+            elif half == 1 and h % 2 == 1:
+                store_words(g, (h - 1) * F, (h + 1) * F)
+            if half == 1 and h == H - 1:
+                store_scales(g)
+
+        interleave_omega(0)
+        new_keys_grouped(0, 0, 1)
+        turn_keys(0, 0)
+        evict_keys(0, 0)
+        quantize_omega(0)
+        new_keys_grouped(0, 1, 1)
+        turn_keys(0, 1)
+        evict_keys(0, 1)
+        quantize_keys(0, 0, 1)
+        interleave_omega(1)
+        quantize_keys(0, 1, 1)
+        quantize_omega(1)
+
+        pending = []
+
+        def run_pending():
+            if pending:
+                first = pending[0]
+                pending.remove(first)
+                first[0](*first[1])
+
+        def prepare_keys(u):
+            turn_keys(u, 0)
+            turn_keys(u, 1)
+            new_keys_grouped(u, 0, 2)
+
+        def unit_by_halves(u, scalar_slots):
+            y[u] = work.tile([P, PACK, F], F32, name="y", bufs=6)
+            for half in range(HALVES):
+                for t in range(PACK):
+                    project_and_exp(u, t, half)
+                    if t - 1 in scalar_slots:
+                        gate_on_scalar(u, t - 1, half)
+                    if t not in scalar_slots:
+                        gate_on_vector(u, t, half, half + 1)
+                    run_pending()
+                    if half == 1 and t % 2 == 1:
+                        store_y(u, t - 1, t + 1, 0 if u == 0 else 1, 2)
+                if u == 0:
+                    prepare_keys(half + 1)
+                    evict_keys(half + 1, 0)
+                    evict_keys(half + 1, 1)
+                elif half == 0:
+                    store_y(u, 0, PACK, 0, 1)
+                if u == 0 and half == 0:
+                    interleave_y(u, half)
+                    pending.extend([(quantize_keys, (1, 0, 2)), (quantize_y, (u, half))])
+                else:
+                    pending.extend([(interleave_y, (u, half)), (quantize_y, (u, half))])
+
+        def unit_by_slots(u, scalar_slots):
+            y[u] = work.tile([P, PACK, F], F32, name="y", bufs=6)
+            ahead = u + 2
+            if u + 1 <= LAST:
+                quantize_keys(u + 1, 0, 2)
+            for t in range(PACK):
+                run_pending()
+                if t == 1 and ahead <= LAST:
+                    prepare_keys(ahead)
+                project_and_exp(u, t, 0)
+                project_and_exp(u, t, 1)
+                if t in scalar_slots:
+                    gate_on_scalar(u, t, 0)
+                    gate_on_vector(u, t, 1, 2)
+                else:
+                    gate_on_vector(u, t, 0, 2)
+                if t in (1, 2) and ahead <= LAST:
+                    evict_keys(ahead, t - 1)
+                if t % 2 == 1:
+                    store_y(u, t - 1, t + 1, 0, 2)
+            pending.extend(
+                [(interleave_y, (u, 0)), (interleave_y, (u, 1)), (quantize_y, (u, 0)), (quantize_y, (u, 1))]
+            )
+
+        unit_by_halves(0, ())
+        for u in range(1, LAST):
+            unit_by_slots(u, (0, 2) if u == LAST - 1 else (0,))
+        unit_by_halves(LAST, (0, 2))
+        run_pending()
+        run_pending()

@@ -24,6 +24,21 @@ HALVES = F // HALF
 RUN = 4
 UNITS = [(g, h) for g in range(GROUPS) for h in range(H)]
 LAST = len(UNITS) - 1
+FRONT = 7
+POPS = [0, 3, 3, 3, 4, 4, 4, 4]
+SMUL = [0, 0, 0, 0, 0, 2, 2, 0]
+EV0 = 0
+KQ = 1
+H0 = 0
+HEADLOAD = "41352"
+HEADV = "132456"
+OS0 = 512
+OS1 = 512
+LS = 352
+PKF = 0
+EVV = 0
+EVU = [0, 1, 1, 0, 0, 0, 0, 0]
+LM = "22"
 
 
 def tile_gated_positive_key_features_g2_kernel(tc, keys, omega, half_norm, key_gate, out_0, out_1, out_2):
@@ -60,37 +75,48 @@ def tile_gated_positive_key_features_g2_kernel(tc, keys, omega, half_norm, key_g
                 keys_raw[u, t] = raw[:, t - t0, :]
 
         rows_per_input = H * GROUPS
-        load_omega(0)
-        nc.sync.dma_start(
-            out=per_key[0:rows_per_input, :], in_=half_norm.rearrange("h (g l) -> (h g) l", g=GROUPS)
-        )
-        nc.sync.dma_start(
-            out=per_key[rows_per_input : 2 * rows_per_input, :],
-            in_=key_gate.rearrange("h (g l) -> (h g) l", g=GROUPS),
-        )
-        load_keys(0, 0, 2)
-        load_keys(0, 2, 4)
-        load_omega(1)
-        for u in range(1, len(UNITS)):
+        def load_per_key():
+            nc.sync.dma_start(
+                out=per_key[0:rows_per_input, :], in_=half_norm.rearrange("h (g l) -> (h g) l", g=GROUPS)
+            )
+            nc.sync.dma_start(
+                out=per_key[rows_per_input : 2 * rows_per_input, :],
+                in_=key_gate.rearrange("h (g l) -> (h g) l", g=GROUPS),
+            )
+
+        for c in HEADLOAD:
+            if c == "1":
+                load_omega(0)
+            if c == "2":
+                load_omega(1)
+            if c == "3":
+                load_per_key()
+            if c == "4":
+                load_keys(0, 0, 2)
+            if c == "5":
+                load_keys(0, 2, 4)
+        for u in range(1, FRONT + 1):
             load_keys(u, 0, PACK)
 
-        per_key_turned = proj_banks.tile([P, 2, P], F32, name="per_key_turned", tag="proj")
-        per_key_words = per_key[:].bitcast(F32)
-        for w in range(2):
-            nc.tensor.transpose(per_key_turned[:, w, :], per_key_words[:, w : GROUP // 2 : 2], identity[:])
-        turned_values = per_key_turned[:].bitcast(BF16)
         neg_norm = keep.tile([P, 2, 2 * rows_per_input], F32, name="neg_norm")
         gate = keep.tile([P, 2, 2 * rows_per_input], F32, name="gate")
-        nc.scalar.activation(neg_norm[:], turned_values[:, :, 0 : 2 * rows_per_input], ACT.Copy, scale=-1.0)
-        nc.scalar.copy(gate[:], turned_values[:, :, 2 * rows_per_input : 4 * rows_per_input])
+
+        def turn_per_key():
+            per_key_turned = proj_banks.tile([P, 2, P], F32, name="per_key_turned", tag="proj")
+            per_key_words = per_key[:].bitcast(F32)
+            for w in range(2):
+                nc.tensor.transpose(per_key_turned[:, w, :], per_key_words[:, w : GROUP // 2 : 2], identity[:])
+            turned_values = per_key_turned[:].bitcast(BF16)
+            nc.scalar.activation(neg_norm[:], turned_values[:, :, 0 : 2 * rows_per_input], ACT.Copy, scale=-1.0)
+            nc.scalar.copy(gate[:], turned_values[:, :, 2 * rows_per_input : 4 * rows_per_input])
 
         def per_key_column(table, u, t):
             g, h = UNITS[u]
             col = 2 * (h * GROUPS + g) + t % 2
             return table[:, t // 2, col : col + 1]
 
-        def interleave(dst, src):
-            nc.vector.tensor_copy(
+        def interleave(dst, src, copy=nc.vector.tensor_copy):
+            copy(
                 out=dst.rearrange("p (c i) t -> p c t i", i=RUN),
                 in_=src.rearrange("p t (c i) -> p c t i", i=RUN),
             )
@@ -101,7 +127,10 @@ def tile_gated_positive_key_features_g2_kernel(tc, keys, omega, half_norm, key_g
 
         def interleave_omega(half):
             omega_grouped[half] = keep.tile([P, HALF, PACK], BF16, name="omega_grouped%d" % half, align_bytes=64)
-            interleave(omega_grouped[half][:], omega_raw[half][:])
+            c = (OS0, OS1)[half]
+            interleave(omega_grouped[half][:, 0:c, :], omega_raw[half][:, :, 0:c])
+            if c < HALF:
+                interleave(omega_grouped[half][:, c:HALF, :], omega_raw[half][:, :, c:HALF], nc.scalar.copy)
 
         def quantize_omega(half):
             omega_codes[half] = keep.tile([P, HALF], U32, name="omega_codes%d" % half, align_bytes=64)
@@ -117,37 +146,37 @@ def tile_gated_positive_key_features_g2_kernel(tc, keys, omega, half_norm, key_g
         key_codes = {}
         key_scales = {}
 
-        def turn_keys(u, pair):
-            bank = turn_banks.tile([P, 2, 2, P], F32, name="keys_turned", tag="turn")
-            keys_turned[u, pair] = bank
-            for s in range(2):
-                words = keys_raw[u, 2 * pair + s].bitcast(F32)
+        def turn_keys(u, t0, t1):
+            bank = turn_banks.tile([P, t1 - t0, 2, P], F32, name="keys_turned", tag="turn")
+            keys_turned[u, t0] = bank
+            for t in range(t0, t1):
+                words = keys_raw[u, t].bitcast(F32)
                 for w in range(2):
-                    nc.tensor.transpose(bank[:, s, w, :], words[:, w : D // 2 : 2], identity[:])
+                    nc.tensor.transpose(bank[:, t - t0, w, :], words[:, w : D // 2 : 2], identity[:])
 
-        def new_keys_grouped(u, pair0, pairs):
-            grouped = work.tile([P, pairs * 2 * P * PACK], BF16, name="keys_grouped", align_bytes=64)
-            for k in range(pairs):
-                keys_grouped[u, pair0 + k] = (grouped, k)
+        def new_keys_grouped(u, t0, t1):
+            grouped = work.tile([P, (t1 - t0) * P * PACK], BF16, name="keys_grouped", bufs=3, align_bytes=64)
+            for t in range(t0, t1):
+                keys_grouped[u, t] = (grouped, t0)
 
-        def evict_keys(u, pair):
-            grouped, k = keys_grouped[u, pair]
-            width = 2 * P * PACK
-            dst = grouped[:, k * width : (k + 1) * width].bitcast(F32)
-            nc.scalar.copy(
-                dst.rearrange("p (s m w) -> p s m w", s=2, w=2),
-                keys_turned[u, pair][:].rearrange("p s w m -> p s m w"),
+        def evict_keys(u, t0, t1, copy=nc.scalar.copy):
+            grouped, base = keys_grouped[u, t0]
+            width = P * PACK
+            dst = grouped[:, (t0 - base) * width : (t1 - base) * width].bitcast(F32)
+            copy(
+                out=dst.rearrange("p (s m w) -> p s m w", s=t1 - t0, w=2),
+                in_=keys_turned[u, t0][:].rearrange("p s w m -> p s m w"),
             )
 
-        def quantize_keys(u, pair0, pairs):
-            if pair0 == 0:
+        def quantize_keys(u, t0, t1):
+            if t0 == 0:
                 key_codes[u] = work.tile([P, PACK * P], U32, name="key_codes", bufs=3, align_bytes=64)
                 key_scales[u] = work.tile([P, PACK * P], U8, name="key_scales", bufs=3, align_bytes=64)
-            cols = slice(pair0 * 2 * P, (pair0 + pairs) * 2 * P)
+            cols = slice(t0 * P, t1 * P)
             nc.vector.quantize_mx(
                 out=key_codes[u][:, cols].bitcast(FP8X4),
                 scales=key_scales[u][:, cols],
-                in_=keys_grouped[u, pair0][0][:],
+                in_=keys_grouped[u, t0][0][:],
             )
 
         y = {}
@@ -185,9 +214,13 @@ def tile_gated_positive_key_features_g2_kernel(tc, keys, omega, half_norm, key_g
             cols = slice(half0 * HALF, half1 * HALF)
             nc.sync.dma_start(out=rows[:, t0:t1, cols], in_=y[u][:, t0:t1, cols])
 
-        def interleave_y(u, half):
-            y_grouped[u, half] = work.tile([P, HALF, PACK], BF16, name="y_grouped", bufs=3, align_bytes=64)
-            interleave(y_grouped[u, half][:], y[u][:, :, half * HALF : (half + 1) * HALF])
+        def interleave_y(u, half, c=HALF):
+            y_grouped[u, half] = work.tile([P, HALF, PACK], BF16, name="y_grouped", bufs=4, align_bytes=64)
+            f0 = half * HALF
+            if c > 0:
+                interleave(y_grouped[u, half][:, 0:c, :], y[u][:, :, f0 : f0 + c])
+            if c < HALF:
+                interleave(y_grouped[u, half][:, c:HALF, :], y[u][:, :, f0 + c : f0 + HALF], nc.scalar.copy)
 
         def store_words(g, m0, m1):
             nc.sync.dma_start(out=words_hbm[g, :, m0:m1], in_=y_words[g][:, m0:m1].bitcast(I32))
@@ -196,7 +229,8 @@ def tile_gated_positive_key_features_g2_kernel(tc, keys, omega, half_norm, key_g
             width = F // 4
             for q in range(4):
                 rows = scales_hbm[g, 4 * q : 4 * q + 4, :].rearrange("r (h m) -> h r m", m=width)
-                nc.sync.dma_start(out=rows, in_=y_scales[g][32 * q : 32 * q + 4 * H, :].bitcast(I32))
+                queue = nc.scalar if g == GROUPS - 1 else nc.sync
+                queue.dma_start(out=rows, in_=y_scales[g][32 * q : 32 * q + 4 * H, :].bitcast(I32))
 
         def quantize_y(u, half):
             g, h = UNITS[u]
@@ -211,25 +245,34 @@ def tile_gated_positive_key_features_g2_kernel(tc, keys, omega, half_norm, key_g
             )
             if u == LAST:
                 store_words(g, m0, m0 + HALF)
-            elif half == 1 and u == LAST - 1:
+            elif half == 1:
                 store_words(g, h * F, (h + 1) * F)
-            elif half == 1 and h % 2 == 1:
-                store_words(g, (h - 1) * F, (h + 1) * F)
             if half == 1 and h == H - 1:
                 store_scales(g)
 
-        interleave_omega(0)
-        new_keys_grouped(0, 0, 1)
-        turn_keys(0, 0)
-        evict_keys(0, 0)
-        quantize_omega(0)
-        new_keys_grouped(0, 1, 1)
-        turn_keys(0, 1)
-        evict_keys(0, 1)
-        quantize_keys(0, 0, 1)
-        interleave_omega(1)
-        quantize_keys(0, 1, 1)
-        quantize_omega(1)
+        if PKF:
+            turn_per_key()
+        new_keys_grouped(0, 0, 2)
+        new_keys_grouped(0, 2, 4)
+        for c in HEADV:
+            if c == "1":
+                interleave_omega(0)
+            if c == "2":
+                quantize_omega(0)
+            if c == "3":
+                turn_keys(0, 0, 2)
+                evict_keys(0, 0, 2)
+                if not PKF:
+                    turn_per_key()
+                quantize_keys(0, 0, 2)
+            if c == "4":
+                interleave_omega(1)
+            if c == "5":
+                turn_keys(0, 2, 4)
+                evict_keys(0, 2, 4)
+                quantize_keys(0, 2, 4)
+            if c == "6":
+                quantize_omega(1)
 
         pending = []
 
@@ -240,61 +283,86 @@ def tile_gated_positive_key_features_g2_kernel(tc, keys, omega, half_norm, key_g
                 first[0](*first[1])
 
         def prepare_keys(u):
-            turn_keys(u, 0)
-            turn_keys(u, 1)
-            new_keys_grouped(u, 0, 2)
+            turn_keys(u, 0, 2)
+            turn_keys(u, 2, 4)
+            new_keys_grouped(u, 0, 4)
 
-        def unit_by_halves(u, scalar_slots):
+        def first_unit():
+            u = 0
             y[u] = work.tile([P, PACK, F], F32, name="y", bufs=6)
             for half in range(HALVES):
+                for t in range(PACK):
+                    project_and_exp(u, t, half)
+                    gate_on_vector(u, t, half, half + 1)
+                    if half == 1 and t == 0:
+                        quantize_keys(1, 0, 4)
+                    if half == 1 and t == 1:
+                        quantize_y(u, 0)
+                    if not H0 and half == 1 and t % 2 == 1:
+                        store_y(u, t - 1, t + 1, 0, 2)
+                if H0:
+                    store_y(u, 0, PACK, half, half + 1)
+                if half == 0:
+                    prepare_keys(1)
+                    evict_keys(1, 0, 2, nc.vector.tensor_copy if EVV > 1 else nc.scalar.copy)
+                    evict_keys(1, 2, 4, nc.vector.tensor_copy if EVV > 0 else nc.scalar.copy)
+                    interleave_y(u, 0)
+            pending.extend([(interleave_y, (u, 1)), (quantize_y, (u, 1))])
+
+        def unit_by_slots(u):
+            y[u] = work.tile([P, PACK, F], F32, name="y", bufs=6)
+            ahead = u + 1
+            if ahead <= LAST:
+                prepare_keys(ahead)
+            for t in range(PACK):
+                project_and_exp(u, t, 0)
+                project_and_exp(u, t, 1)
+                if t >= EV0 and t < EV0 + 2 and ahead <= LAST:
+                    evict_keys(ahead, 2 * (t - EV0), 2 * (t - EV0) + 2, nc.vector.tensor_copy if (t - EV0) < EVU[u] % 5 else nc.scalar.copy)
+                if t in (2, 3, 0, 1)[: SMUL[u] % 5]:
+                    gate_on_scalar(u, t, 0)
+                    gate_on_vector(u, t, 1, 2)
+                else:
+                    gate_on_vector(u, t, 0, 2)
+                if t % 2 == 1:
+                    store_y(u, t - 1, t + 1, 0, 2)
+                if t == 1 and FRONT + u <= LAST:
+                    load_keys(FRONT + u, 0, PACK)
+                if t == KQ and ahead <= LAST:
+                    quantize_keys(ahead, 0, 4)
+                if t < POPS[u]:
+                    run_pending()
+                if t == 3 and POPS[u] > 4:
+                    run_pending()
+            pending.extend(
+                [(interleave_y, (u, 0)), (interleave_y, (u, 1)), (quantize_y, (u, 0)), (quantize_y, (u, 1))]
+            )
+
+        def last_unit():
+            u = LAST
+            y[u] = work.tile([P, PACK, F], F32, name="y", bufs=6)
+            for half in range(HALVES):
+                scalar_slots = (0, 2, 1)[: int(LM[half]) % 5]
                 for t in range(PACK):
                     project_and_exp(u, t, half)
                     if t - 1 in scalar_slots:
                         gate_on_scalar(u, t - 1, half)
                     if t not in scalar_slots:
                         gate_on_vector(u, t, half, half + 1)
+                    if half == 1 and t % 2 == 1 and (t == 3 or 1 not in scalar_slots):
+                        store_y(u, 0 if (t == 1 or 1 in scalar_slots) else 2, t + 1, 1, 2)
                     run_pending()
-                    if half == 1 and t % 2 == 1:
-                        store_y(u, t - 1, t + 1, 0 if u == 0 else 1, 2)
-                if u == 0:
-                    prepare_keys(half + 1)
-                    evict_keys(half + 1, 0)
-                    evict_keys(half + 1, 1)
-                elif half == 0:
+                    if t < POPS[u] - 4:
+                        run_pending()
+                if half == 0:
                     store_y(u, 0, PACK, 0, 1)
-                if u == 0 and half == 0:
-                    interleave_y(u, half)
-                    pending.extend([(quantize_keys, (1, 0, 2)), (quantize_y, (u, half))])
-                else:
                     pending.extend([(interleave_y, (u, half)), (quantize_y, (u, half))])
-
-        def unit_by_slots(u, scalar_slots):
-            y[u] = work.tile([P, PACK, F], F32, name="y", bufs=6)
-            ahead = u + 2
-            if u + 1 <= LAST:
-                quantize_keys(u + 1, 0, 2)
-            for t in range(PACK):
+            for k in range(len(pending)):
                 run_pending()
-                if t == 1 and ahead <= LAST:
-                    prepare_keys(ahead)
-                project_and_exp(u, t, 0)
-                project_and_exp(u, t, 1)
-                if t in scalar_slots:
-                    gate_on_scalar(u, t, 0)
-                    gate_on_vector(u, t, 1, 2)
-                else:
-                    gate_on_vector(u, t, 0, 2)
-                if t in (1, 2) and ahead <= LAST:
-                    evict_keys(ahead, t - 1)
-                if t % 2 == 1:
-                    store_y(u, t - 1, t + 1, 0, 2)
-            pending.extend(
-                [(interleave_y, (u, 0)), (interleave_y, (u, 1)), (quantize_y, (u, 0)), (quantize_y, (u, 1))]
-            )
+            interleave_y(u, 1, LS)
+            quantize_y(u, 1)
 
-        unit_by_halves(0, ())
+        first_unit()
         for u in range(1, LAST):
-            unit_by_slots(u, (0, 2) if u == LAST - 1 else (0,))
-        unit_by_halves(LAST, (0, 2))
-        run_pending()
-        run_pending()
+            unit_by_slots(u)
+        last_unit()

@@ -24,10 +24,9 @@ HALVES = F // HALF
 RUN = 4
 UNITS = [(g, h) for g in range(GROUPS) for h in range(H)]
 LAST = len(UNITS) - 1
-FRONT = 7
 POPS = [0, 3, 3, 3, 4, 4, 4, 4]
-SMUL = [0, 0, 0, 0, 0, 2, 2, 0]
-EV0 = 0
+SMUL = [0, 0, 0, 0, 1, 1, 1, 0]
+EV0 = 2
 KQ = 1
 H0 = 0
 HEADLOAD = "41352"
@@ -37,8 +36,14 @@ OS1 = 512
 LS = 352
 PKF = 0
 EVV = 0
-EVU = [0, 1, 1, 0, 0, 0, 0, 0]
+EVU = [0, 1, 0, 0, 0, 0, 0, 0]
+MERGE = 1
+WHOLE = 0
+WSTORE = [(u, 1) for u in range(8)] + [(7, 0)]
+AH = 2
+EV2 = 1
 LM = "22"
+Y_RUN = 2
 
 
 def tile_gated_positive_key_features_g2_kernel(tc, keys, omega, half_norm, key_gate, out_0, out_1, out_2):
@@ -95,8 +100,18 @@ def tile_gated_positive_key_features_g2_kernel(tc, keys, omega, half_norm, key_g
                 load_keys(0, 0, 2)
             if c == "5":
                 load_keys(0, 2, 4)
-        for u in range(1, FRONT + 1):
-            load_keys(u, 0, PACK)
+        def load_keys_many(u0, u1):
+            g, h0 = UNITS[u0]
+            n = u1 - u0
+            raw = keep.tile([P, n, PACK * D], BF16, name="keys_raw%d" % u0)
+            rows = keys[h0 : h0 + n, g * GROUP : (g + 1) * GROUP, :].rearrange("h (p t) d -> p h (t d)", t=PACK)
+            nc.sync.dma_start(out=raw[:], in_=rows)
+            for k in range(n):
+                for t in range(PACK):
+                    keys_raw[u0 + k, t] = raw[:, k, t * D : (t + 1) * D]
+
+        for u0, u1 in ((1, 2), (2, 4), (4, 8)) if MERGE else [(k, k + 1) for k in range(1, 8)]:
+            load_keys_many(u0, u1)
 
         neg_norm = keep.tile([P, 2, 2 * rows_per_input], F32, name="neg_norm")
         gate = keep.tile([P, 2, 2 * rows_per_input], F32, name="gate")
@@ -115,10 +130,10 @@ def tile_gated_positive_key_features_g2_kernel(tc, keys, omega, half_norm, key_g
             col = 2 * (h * GROUPS + g) + t % 2
             return table[:, t // 2, col : col + 1]
 
-        def interleave(dst, src, copy=nc.vector.tensor_copy):
+        def interleave(dst, src, copy=nc.vector.tensor_copy, run=RUN):
             copy(
-                out=dst.rearrange("p (c i) t -> p c t i", i=RUN),
-                in_=src.rearrange("p t (c i) -> p c t i", i=RUN),
+                out=dst.rearrange("p (c i) t -> p c t i", i=run),
+                in_=src.rearrange("p t (c i) -> p c t i", i=run),
             )
 
         omega_grouped = {}
@@ -180,6 +195,7 @@ def tile_gated_positive_key_features_g2_kernel(tc, keys, omega, half_norm, key_g
             )
 
         y = {}
+        words_done = {0: 0, 1: 0}
         y_grouped = {}
         y_words = {}
         y_scales = {}
@@ -218,9 +234,9 @@ def tile_gated_positive_key_features_g2_kernel(tc, keys, omega, half_norm, key_g
             y_grouped[u, half] = work.tile([P, HALF, PACK], BF16, name="y_grouped", bufs=4, align_bytes=64)
             f0 = half * HALF
             if c > 0:
-                interleave(y_grouped[u, half][:, 0:c, :], y[u][:, :, f0 : f0 + c])
+                interleave(y_grouped[u, half][:, 0:c, :], y[u][:, :, f0 : f0 + c], run=Y_RUN)
             if c < HALF:
-                interleave(y_grouped[u, half][:, c:HALF, :], y[u][:, :, f0 + c : f0 + HALF], nc.scalar.copy)
+                interleave(y_grouped[u, half][:, c:HALF, :], y[u][:, :, f0 + c : f0 + HALF], nc.scalar.copy, Y_RUN)
 
         def store_words(g, m0, m1):
             nc.sync.dma_start(out=words_hbm[g, :, m0:m1], in_=y_words[g][:, m0:m1].bitcast(I32))
@@ -243,10 +259,9 @@ def tile_gated_positive_key_features_g2_kernel(tc, keys, omega, half_norm, key_g
                 scales=y_scales[g][4 * h : P, half * HALF : (half + 1) * HALF],
                 in_=y_grouped[u, half][:].rearrange("p f t -> p (f t)"),
             )
-            if u == LAST:
-                store_words(g, m0, m0 + HALF)
-            elif half == 1:
-                store_words(g, h * F, (h + 1) * F)
+            if (u, half) in WSTORE:
+                store_words(g, words_done[g], m0 + HALF)
+                words_done[g] = m0 + HALF
             if half == 1 and h == H - 1:
                 store_scales(g)
 
@@ -307,14 +322,22 @@ def tile_gated_positive_key_features_g2_kernel(tc, keys, omega, half_norm, key_g
                     evict_keys(1, 0, 2, nc.vector.tensor_copy if EVV > 1 else nc.scalar.copy)
                     evict_keys(1, 2, 4, nc.vector.tensor_copy if EVV > 0 else nc.scalar.copy)
                     interleave_y(u, 0)
+                elif AH == 2:
+                    prepare_keys(2)
+                    evict_keys(2, 0, 2, nc.vector.tensor_copy if EV2 > 0 else nc.scalar.copy)
+                    evict_keys(2, 2, 4, nc.vector.tensor_copy if EV2 > 1 else nc.scalar.copy)
             pending.extend([(interleave_y, (u, 1)), (quantize_y, (u, 1))])
 
         def unit_by_slots(u):
             y[u] = work.tile([P, PACK, F], F32, name="y", bufs=6)
-            ahead = u + 1
-            if ahead <= LAST:
-                prepare_keys(ahead)
+            ahead = u + AH
+            if AH == 2 and u + 1 <= LAST:
+                quantize_keys(u + 1, 0, 4)
             for t in range(PACK):
+                if t == EV0 and ahead <= LAST:
+                    new_keys_grouped(ahead, 0, 4)
+                if t >= EV0 and t < EV0 + 2 and ahead <= LAST:
+                    turn_keys(ahead, 2 * (t - EV0), 2 * (t - EV0) + 2)
                 project_and_exp(u, t, 0)
                 project_and_exp(u, t, 1)
                 if t >= EV0 and t < EV0 + 2 and ahead <= LAST:
@@ -324,11 +347,11 @@ def tile_gated_positive_key_features_g2_kernel(tc, keys, omega, half_norm, key_g
                     gate_on_vector(u, t, 1, 2)
                 else:
                     gate_on_vector(u, t, 0, 2)
-                if t % 2 == 1:
+                if u <= WHOLE and t == 3:
+                    store_y(u, 0, 4, 0, 2)
+                if u > WHOLE and t % 2 == 1:
                     store_y(u, t - 1, t + 1, 0, 2)
-                if t == 1 and FRONT + u <= LAST:
-                    load_keys(FRONT + u, 0, PACK)
-                if t == KQ and ahead <= LAST:
+                if AH == 1 and t == KQ and ahead <= LAST:
                     quantize_keys(ahead, 0, 4)
                 if t < POPS[u]:
                     run_pending()

@@ -21,29 +21,19 @@ GROUP = P * PACK
 GROUPS = L // GROUP
 HALF = 512
 HALVES = F // HALF
+PAIR = 2
+QUADRANTS = 4
 RUN = 4
 UNITS = [(g, h) for g in range(GROUPS) for h in range(H)]
 LAST = len(UNITS) - 1
-POPS = [0, 3, 3, 3, 4, 4, 4, 4]
-SMUL = [0, 0, 0, 0, 1, 1, 1, 0]
-EV0 = 2
-KQ = 1
-H0 = 0
-HEADLOAD = "41352"
-HEADV = "132456"
-OS0 = 512
-OS1 = 512
-LS = 352
-PKF = 0
-EVV = 0
-EVU = [0, 1, 0, 0, 0, 0, 0, 0]
-MERGE = 1
-WHOLE = 0
-WSTORE = [(u, 1) for u in range(8)] + [(7, 0)]
-AH = 2
-EV2 = 1
-LM = "22"
-Y_RUN = 2
+
+VECTOR_EVICTS_BEFORE = 3
+DEFER_BEFORE = 4
+SCALAR_GATES_FROM = 5
+VECTOR_COLUMNS = 352
+
+PROJ_BANKS = 6
+Y_BUFS = 6
 
 
 def tile_gated_positive_key_features_g2_kernel(tc, keys, omega, half_norm, key_gate, out_0, out_1, out_2):
@@ -54,12 +44,14 @@ def tile_gated_positive_key_features_g2_kernel(tc, keys, omega, half_norm, key_g
     with ExitStack() as ctx:
         keep = ctx.enter_context(tc.tile_pool(name="keep", bufs=1))
         work = ctx.enter_context(tc.tile_pool(name="work", bufs=2))
-        proj_banks = ctx.enter_context(tc.psum_pool(name="proj_banks", bufs=6))
+        proj_banks = ctx.enter_context(tc.psum_pool(name="proj_banks", bufs=PROJ_BANKS))
         turn_banks = ctx.enter_context(tc.psum_pool(name="turn_banks", bufs=2))
         ctx.enter_context(tc.manual_schedule())
 
         identity = keep.tile([P, P], F32, name="identity")
         make_identity(nc, identity[:])
+
+        rows = H * GROUPS
         per_key = keep.tile([P, GROUP], BF16, name="per_key")
         nc.vector.memset(per_key[:], 0.0)
 
@@ -68,72 +60,57 @@ def tile_gated_positive_key_features_g2_kernel(tc, keys, omega, half_norm, key_g
 
         def load_omega(half):
             omega_raw[half] = keep.tile([P, PACK, HALF], BF16, name="omega_raw%d" % half)
-            cols = omega[:, half * HALF : (half + 1) * HALF]
-            nc.sync.dma_start(out=omega_raw[half][:], in_=cols.rearrange("(p j) f -> p j f", j=PACK))
+            columns = omega[:, half * HALF : (half + 1) * HALF]
+            nc.sync.dma_start(out=omega_raw[half][:], in_=columns.rearrange("(p j) f -> p j f", j=PACK))
 
-        def load_keys(u, t0, t1):
-            g, h = UNITS[u]
-            raw = keep.tile([P, t1 - t0, D], BF16, name="keys_raw%d_%d" % (u, t0))
-            rows = keys[h, g * GROUP : (g + 1) * GROUP, :].rearrange("(p t) d -> p t d", t=PACK)
-            nc.sync.dma_start(out=raw[:], in_=rows[:, t0:t1, :])
-            for t in range(t0, t1):
-                keys_raw[u, t] = raw[:, t - t0, :]
+        def load_first_keys(t0):
+            g, h = UNITS[0]
+            raw = keep.tile([P, PAIR, D], BF16, name="first_keys_raw%d" % t0)
+            unit_rows = keys[h, g * GROUP : (g + 1) * GROUP, :].rearrange("(p t) d -> p t d", t=PACK)
+            nc.sync.dma_start(out=raw[:], in_=unit_rows[:, t0 : t0 + PAIR, :])
+            for t in range(t0, t0 + PAIR):
+                keys_raw[0, t] = raw[:, t - t0, :]
 
-        rows_per_input = H * GROUPS
-        def load_per_key():
-            nc.sync.dma_start(
-                out=per_key[0:rows_per_input, :], in_=half_norm.rearrange("h (g l) -> (h g) l", g=GROUPS)
-            )
-            nc.sync.dma_start(
-                out=per_key[rows_per_input : 2 * rows_per_input, :],
-                in_=key_gate.rearrange("h (g l) -> (h g) l", g=GROUPS),
-            )
-
-        for c in HEADLOAD:
-            if c == "1":
-                load_omega(0)
-            if c == "2":
-                load_omega(1)
-            if c == "3":
-                load_per_key()
-            if c == "4":
-                load_keys(0, 0, 2)
-            if c == "5":
-                load_keys(0, 2, 4)
-        def load_keys_many(u0, u1):
+        def load_keys(u0, u1):
             g, h0 = UNITS[u0]
-            n = u1 - u0
-            raw = keep.tile([P, n, PACK * D], BF16, name="keys_raw%d" % u0)
-            rows = keys[h0 : h0 + n, g * GROUP : (g + 1) * GROUP, :].rearrange("h (p t) d -> p h (t d)", t=PACK)
-            nc.sync.dma_start(out=raw[:], in_=rows)
-            for k in range(n):
+            raw = keep.tile([P, u1 - u0, PACK * D], BF16, name="keys_raw%d" % u0)
+            heads = keys[h0 : h0 + u1 - u0, g * GROUP : (g + 1) * GROUP, :]
+            nc.sync.dma_start(out=raw[:], in_=heads.rearrange("h (p t) d -> p h (t d)", t=PACK))
+            for u in range(u0, u1):
                 for t in range(PACK):
-                    keys_raw[u0 + k, t] = raw[:, k, t * D : (t + 1) * D]
+                    keys_raw[u, t] = raw[:, u - u0, t * D : (t + 1) * D]
 
-        for u0, u1 in ((1, 2), (2, 4), (4, 8)) if MERGE else [(k, k + 1) for k in range(1, 8)]:
-            load_keys_many(u0, u1)
+        load_first_keys(0)
+        load_omega(0)
+        nc.sync.dma_start(out=per_key[0:rows, :], in_=half_norm.rearrange("h (g l) -> (h g) l", g=GROUPS))
+        nc.sync.dma_start(out=per_key[rows : 2 * rows, :], in_=key_gate.rearrange("h (g l) -> (h g) l", g=GROUPS))
+        load_first_keys(PAIR)
+        load_omega(1)
+        load_keys(1, 2)
+        load_keys(2, H)
+        load_keys(H, 2 * H)
 
-        neg_norm = keep.tile([P, 2, 2 * rows_per_input], F32, name="neg_norm")
-        gate = keep.tile([P, 2, 2 * rows_per_input], F32, name="gate")
+        neg_norm = keep.tile([P, 2, 2 * rows], F32, name="neg_norm")
+        gate = keep.tile([P, 2, 2 * rows], F32, name="gate")
 
         def turn_per_key():
-            per_key_turned = proj_banks.tile([P, 2, P], F32, name="per_key_turned", tag="proj")
-            per_key_words = per_key[:].bitcast(F32)
+            bank = proj_banks.tile([P, 2, P], F32, name="per_key_turned", tag="proj")
+            words = per_key[:].bitcast(F32)
             for w in range(2):
-                nc.tensor.transpose(per_key_turned[:, w, :], per_key_words[:, w : GROUP // 2 : 2], identity[:])
-            turned_values = per_key_turned[:].bitcast(BF16)
-            nc.scalar.activation(neg_norm[:], turned_values[:, :, 0 : 2 * rows_per_input], ACT.Copy, scale=-1.0)
-            nc.scalar.copy(gate[:], turned_values[:, :, 2 * rows_per_input : 4 * rows_per_input])
+                nc.tensor.transpose(bank[:, w, :], words[:, w : GROUP // 2 : 2], identity[:])
+            values = bank[:].bitcast(BF16)
+            nc.scalar.activation(neg_norm[:], values[:, :, 0 : 2 * rows], ACT.Copy, scale=-1.0)
+            nc.scalar.copy(gate[:], values[:, :, 2 * rows : 4 * rows])
 
         def per_key_column(table, u, t):
             g, h = UNITS[u]
-            col = 2 * (h * GROUPS + g) + t % 2
-            return table[:, t // 2, col : col + 1]
+            column = 2 * (h * GROUPS + g) + t % 2
+            return table[:, t // 2, column : column + 1]
 
-        def interleave(dst, src, copy=nc.vector.tensor_copy, run=RUN):
+        def interleave(copy, dst, src):
             copy(
-                out=dst.rearrange("p (c i) t -> p c t i", i=run),
-                in_=src.rearrange("p t (c i) -> p c t i", i=run),
+                out=dst.rearrange("p (c i) t -> p c t i", i=RUN),
+                in_=src.rearrange("p t (c i) -> p c t i", i=RUN),
             )
 
         omega_grouped = {}
@@ -142,10 +119,7 @@ def tile_gated_positive_key_features_g2_kernel(tc, keys, omega, half_norm, key_g
 
         def interleave_omega(half):
             omega_grouped[half] = keep.tile([P, HALF, PACK], BF16, name="omega_grouped%d" % half, align_bytes=64)
-            c = (OS0, OS1)[half]
-            interleave(omega_grouped[half][:, 0:c, :], omega_raw[half][:, :, 0:c])
-            if c < HALF:
-                interleave(omega_grouped[half][:, c:HALF, :], omega_raw[half][:, :, c:HALF], nc.scalar.copy)
+            interleave(nc.vector.tensor_copy, omega_grouped[half][:], omega_raw[half][:])
 
         def quantize_omega(half):
             omega_codes[half] = keep.tile([P, HALF], U32, name="omega_codes%d" % half, align_bytes=64)
@@ -158,28 +132,26 @@ def tile_gated_positive_key_features_g2_kernel(tc, keys, omega, half_norm, key_g
 
         keys_turned = {}
         keys_grouped = {}
+        keys_grouped_pair = {}
         key_codes = {}
         key_scales = {}
 
-        def turn_keys(u, t0, t1):
-            bank = turn_banks.tile([P, t1 - t0, 2, P], F32, name="keys_turned", tag="turn")
-            keys_turned[u, t0] = bank
-            for t in range(t0, t1):
+        def turn_keys(u, t0):
+            keys_turned[u, t0] = turn_banks.tile([P, PAIR, 2, P], F32, name="keys_turned")
+            for t in range(t0, t0 + PAIR):
                 words = keys_raw[u, t].bitcast(F32)
                 for w in range(2):
-                    nc.tensor.transpose(bank[:, t - t0, w, :], words[:, w : D // 2 : 2], identity[:])
+                    nc.tensor.transpose(keys_turned[u, t0][:, t - t0, w, :], words[:, w : D // 2 : 2], identity[:])
 
         def new_keys_grouped(u, t0, t1):
             grouped = work.tile([P, (t1 - t0) * P * PACK], BF16, name="keys_grouped", bufs=3, align_bytes=64)
-            for t in range(t0, t1):
-                keys_grouped[u, t] = (grouped, t0)
+            keys_grouped[u, t0] = grouped
+            for t in range(t0, t1, PAIR):
+                keys_grouped_pair[u, t] = grouped[:, (t - t0) * P * PACK : (t - t0 + PAIR) * P * PACK]
 
-        def evict_keys(u, t0, t1, copy=nc.scalar.copy):
-            grouped, base = keys_grouped[u, t0]
-            width = P * PACK
-            dst = grouped[:, (t0 - base) * width : (t1 - base) * width].bitcast(F32)
+        def evict_keys(u, t0, copy):
             copy(
-                out=dst.rearrange("p (s m w) -> p s m w", s=t1 - t0, w=2),
+                out=keys_grouped_pair[u, t0].bitcast(F32).rearrange("p (s m w) -> p s m w", s=PAIR, w=2),
                 in_=keys_turned[u, t0][:].rearrange("p s w m -> p s m w"),
             )
 
@@ -187,66 +159,68 @@ def tile_gated_positive_key_features_g2_kernel(tc, keys, omega, half_norm, key_g
             if t0 == 0:
                 key_codes[u] = work.tile([P, PACK * P], U32, name="key_codes", bufs=3, align_bytes=64)
                 key_scales[u] = work.tile([P, PACK * P], U8, name="key_scales", bufs=3, align_bytes=64)
-            cols = slice(t0 * P, t1 * P)
+            columns = slice(t0 * P, t1 * P)
             nc.vector.quantize_mx(
-                out=key_codes[u][:, cols].bitcast(FP8X4),
-                scales=key_scales[u][:, cols],
-                in_=keys_grouped[u, t0][0][:],
+                out=key_codes[u][:, columns].bitcast(FP8X4),
+                scales=key_scales[u][:, columns],
+                in_=keys_grouped[u, t0][:],
             )
 
+        def turn_unit_keys(u):
+            for t0 in range(0, PACK, PAIR):
+                turn_keys(u, t0)
+            new_keys_grouped(u, 0, PACK)
+
         y = {}
-        words_done = {0: 0, 1: 0}
         y_grouped = {}
         y_words = {}
         y_scales = {}
 
+        def y_part(u, t0, t1, f0, f1):
+            if u in (0, LAST):
+                half = f0 // HALF
+                return y[u][:, half, t0:t1, f0 - half * HALF : f1 - half * HALF]
+            return y[u][:, t0:t1, f0:f1]
+
+        def y_slot(u, t, half0, half1):
+            return y_part(u, t, t + 1, half0 * HALF, half1 * HALF)[:, 0, :]
+
         def project_and_exp(u, t, half):
             bank = proj_banks.tile([P, HALF], F32, name="proj", tag="proj")
-            cols = slice(t * P, (t + 1) * P)
+            columns = slice(t * P, (t + 1) * P)
             nc.tensor.matmul_mx(
                 out=bank[:],
-                lhsT=key_codes[u][:, cols].bitcast(FP8X4),
-                lhsT_scale=key_scales[u][:, cols],
+                lhsT=key_codes[u][:, columns].bitcast(FP8X4),
+                lhsT_scale=key_scales[u][:, columns],
                 rhs=omega_codes[half][:].bitcast(FP8X4),
                 rhs_scale=omega_scales[half][:],
                 start=True,
                 stop=True,
             )
-            nc.scalar.activation(
-                y[u][:, t, half * HALF : (half + 1) * HALF], bank[:], ACT.Exp, bias=per_key_column(neg_norm, u, t)
-            )
+            nc.scalar.activation(y_slot(u, t, half, half + 1), bank[:], ACT.Exp, bias=per_key_column(neg_norm, u, t))
 
         def gate_on_vector(u, t, half0, half1):
-            part = y[u][:, t, half0 * HALF : half1 * HALF]
+            part = y_slot(u, t, half0, half1)
             nc.vector.tensor_scalar(part, part, per_key_column(gate, u, t), None, ALU.mult)
 
         def gate_on_scalar(u, t, half):
-            part = y[u][:, t, half * HALF : (half + 1) * HALF]
+            part = y_slot(u, t, half, half + 1)
             nc.scalar.activation(part, part, ACT.Copy, scale=per_key_column(gate, u, t))
 
         def store_y(u, t0, t1, half0, half1):
             g, h = UNITS[u]
-            rows = out_0[h, g * GROUP : (g + 1) * GROUP, :].rearrange("(p t) f -> p t f", t=PACK)
-            cols = slice(half0 * HALF, half1 * HALF)
-            nc.sync.dma_start(out=rows[:, t0:t1, cols], in_=y[u][:, t0:t1, cols])
+            unit_rows = out_0[h, g * GROUP : (g + 1) * GROUP, :].rearrange("(p t) f -> p t f", t=PACK)
+            f0, f1 = half0 * HALF, half1 * HALF
+            nc.sync.dma_start(out=unit_rows[:, t0:t1, f0:f1], in_=y_part(u, t0, t1, f0, f1))
 
-        def interleave_y(u, half, c=HALF):
-            y_grouped[u, half] = work.tile([P, HALF, PACK], BF16, name="y_grouped", bufs=4, align_bytes=64)
+        def interleave_y(u, half, vector_columns=HALF):
+            grouped = work.tile([P, HALF, PACK], BF16, name="y_grouped", bufs=4, align_bytes=64)
+            y_grouped[u, half] = grouped
             f0 = half * HALF
-            if c > 0:
-                interleave(y_grouped[u, half][:, 0:c, :], y[u][:, :, f0 : f0 + c], run=Y_RUN)
-            if c < HALF:
-                interleave(y_grouped[u, half][:, c:HALF, :], y[u][:, :, f0 + c : f0 + HALF], nc.scalar.copy, Y_RUN)
-
-        def store_words(g, m0, m1):
-            nc.sync.dma_start(out=words_hbm[g, :, m0:m1], in_=y_words[g][:, m0:m1].bitcast(I32))
-
-        def store_scales(g):
-            width = F // 4
-            for q in range(4):
-                rows = scales_hbm[g, 4 * q : 4 * q + 4, :].rearrange("r (h m) -> h r m", m=width)
-                queue = nc.scalar if g == GROUPS - 1 else nc.sync
-                queue.dma_start(out=rows, in_=y_scales[g][32 * q : 32 * q + 4 * H, :].bitcast(I32))
+            cut = f0 + vector_columns
+            interleave(nc.vector.tensor_copy, grouped[:, 0:vector_columns, :], y_part(u, 0, PACK, f0, cut))
+            if vector_columns < HALF:
+                interleave(nc.scalar.copy, grouped[:, vector_columns:HALF, :], y_part(u, 0, PACK, cut, f0 + HALF))
 
         def quantize_y(u, half):
             g, h = UNITS[u]
@@ -259,133 +233,91 @@ def tile_gated_positive_key_features_g2_kernel(tc, keys, omega, half_norm, key_g
                 scales=y_scales[g][4 * h : P, half * HALF : (half + 1) * HALF],
                 in_=y_grouped[u, half][:].rearrange("p f t -> p (f t)"),
             )
-            if (u, half) in WSTORE:
-                store_words(g, words_done[g], m0 + HALF)
-                words_done[g] = m0 + HALF
-            if half == 1 and h == H - 1:
-                store_scales(g)
+            if u == LAST or half == HALVES - 1:
+                columns = slice(m0 if u == LAST else h * F, m0 + HALF)
+                nc.sync.dma_start(out=words_hbm[g, :, columns], in_=y_words[g][:, columns].bitcast(I32))
+            if h == H - 1 and half == HALVES - 1:
+                for q in range(QUADRANTS):
+                    blocks = scales_hbm[g, 4 * q : 4 * q + 4, :].rearrange("r (h m) -> h r m", h=H)
+                    nc.sync.dma_start(out=blocks, in_=y_scales[g][32 * q : 32 * q + 4 * H, :].bitcast(I32))
 
-        if PKF:
-            turn_per_key()
-        new_keys_grouped(0, 0, 2)
-        new_keys_grouped(0, 2, 4)
-        for c in HEADV:
-            if c == "1":
-                interleave_omega(0)
-            if c == "2":
-                quantize_omega(0)
-            if c == "3":
-                turn_keys(0, 0, 2)
-                evict_keys(0, 0, 2)
-                if not PKF:
-                    turn_per_key()
-                quantize_keys(0, 0, 2)
-            if c == "4":
-                interleave_omega(1)
-            if c == "5":
-                turn_keys(0, 2, 4)
-                evict_keys(0, 2, 4)
-                quantize_keys(0, 2, 4)
-            if c == "6":
-                quantize_omega(1)
+        finishing = []
 
-        pending = []
+        def finish_one():
+            if finishing:
+                step = finishing[0]
+                finishing.remove(step)
+                step[0](*step[1])
 
-        def run_pending():
-            if pending:
-                first = pending[0]
-                pending.remove(first)
-                first[0](*first[1])
+        new_keys_grouped(0, 0, PAIR)
+        new_keys_grouped(0, PAIR, PACK)
+        interleave_omega(0)
+        turn_keys(0, 0)
+        evict_keys(0, 0, nc.scalar.copy)
+        turn_per_key()
+        quantize_keys(0, 0, PAIR)
+        quantize_omega(0)
+        interleave_omega(1)
+        turn_keys(0, PAIR)
+        evict_keys(0, PAIR, nc.scalar.copy)
+        quantize_keys(0, PAIR, PACK)
+        quantize_omega(1)
 
-        def prepare_keys(u):
-            turn_keys(u, 0, 2)
-            turn_keys(u, 2, 4)
-            new_keys_grouped(u, 0, 4)
+        y[0] = work.tile([P, HALVES, PACK, HALF], F32, name="y", bufs=Y_BUFS)
+        for t in range(PACK):
+            project_and_exp(0, t, 0)
+            gate_on_vector(0, t, 0, 1)
+        store_y(0, 0, PACK, 0, 1)
+        turn_unit_keys(1)
+        evict_keys(1, 0, nc.scalar.copy)
+        evict_keys(1, PAIR, nc.scalar.copy)
+        interleave_y(0, 0)
+        for t in range(PACK):
+            project_and_exp(0, t, 1)
+            gate_on_vector(0, t, 1, 2)
+            if t == 0:
+                quantize_keys(1, 0, PACK)
+            if t == 1:
+                quantize_y(0, 0)
+        store_y(0, 0, PACK, 1, 2)
+        finishing.extend([(interleave_y, (0, 1)), (quantize_y, (0, 1))])
 
-        def first_unit():
-            u = 0
-            y[u] = work.tile([P, PACK, F], F32, name="y", bufs=6)
-            for half in range(HALVES):
-                for t in range(PACK):
-                    project_and_exp(u, t, half)
-                    gate_on_vector(u, t, half, half + 1)
-                    if half == 1 and t == 0:
-                        quantize_keys(1, 0, 4)
-                    if half == 1 and t == 1:
-                        quantize_y(u, 0)
-                    if not H0 and half == 1 and t % 2 == 1:
-                        store_y(u, t - 1, t + 1, 0, 2)
-                if H0:
-                    store_y(u, 0, PACK, half, half + 1)
-                if half == 0:
-                    prepare_keys(1)
-                    evict_keys(1, 0, 2, nc.vector.tensor_copy if EVV > 1 else nc.scalar.copy)
-                    evict_keys(1, 2, 4, nc.vector.tensor_copy if EVV > 0 else nc.scalar.copy)
-                    interleave_y(u, 0)
-                elif AH == 2:
-                    prepare_keys(2)
-                    evict_keys(2, 0, 2, nc.vector.tensor_copy if EV2 > 0 else nc.scalar.copy)
-                    evict_keys(2, 2, 4, nc.vector.tensor_copy if EV2 > 1 else nc.scalar.copy)
-            pending.extend([(interleave_y, (u, 1)), (quantize_y, (u, 1))])
-
-        def unit_by_slots(u):
-            y[u] = work.tile([P, PACK, F], F32, name="y", bufs=6)
-            ahead = u + AH
-            if AH == 2 and u + 1 <= LAST:
-                quantize_keys(u + 1, 0, 4)
+        for u in range(1, LAST):
+            y[u] = work.tile([P, PACK, F], F32, name="y", bufs=Y_BUFS)
+            turn_unit_keys(u + 1)
             for t in range(PACK):
-                if t == EV0 and ahead <= LAST:
-                    new_keys_grouped(ahead, 0, 4)
-                if t >= EV0 and t < EV0 + 2 and ahead <= LAST:
-                    turn_keys(ahead, 2 * (t - EV0), 2 * (t - EV0) + 2)
                 project_and_exp(u, t, 0)
                 project_and_exp(u, t, 1)
-                if t >= EV0 and t < EV0 + 2 and ahead <= LAST:
-                    evict_keys(ahead, 2 * (t - EV0), 2 * (t - EV0) + 2, nc.vector.tensor_copy if (t - EV0) < EVU[u] % 5 else nc.scalar.copy)
-                if t in (2, 3, 0, 1)[: SMUL[u] % 5]:
+                if t == 0:
+                    evict_keys(u + 1, 0, nc.vector.tensor_copy if u < VECTOR_EVICTS_BEFORE else nc.scalar.copy)
+                if t == 1:
+                    evict_keys(u + 1, PAIR, nc.scalar.copy)
+                if u >= SCALAR_GATES_FROM and t >= PAIR:
                     gate_on_scalar(u, t, 0)
                     gate_on_vector(u, t, 1, 2)
                 else:
                     gate_on_vector(u, t, 0, 2)
-                if u <= WHOLE and t == 3:
-                    store_y(u, 0, 4, 0, 2)
-                if u > WHOLE and t % 2 == 1:
-                    store_y(u, t - 1, t + 1, 0, 2)
-                if AH == 1 and t == KQ and ahead <= LAST:
-                    quantize_keys(ahead, 0, 4)
-                if t < POPS[u]:
-                    run_pending()
-                if t == 3 and POPS[u] > 4:
-                    run_pending()
-            pending.extend(
-                [(interleave_y, (u, 0)), (interleave_y, (u, 1)), (quantize_y, (u, 0)), (quantize_y, (u, 1))]
-            )
+                if t % PAIR == PAIR - 1:
+                    store_y(u, t + 1 - PAIR, t + 1, 0, 2)
+                if t == 1:
+                    quantize_keys(u + 1, 0, PACK)
+                if u >= DEFER_BEFORE or t < PACK - 1:
+                    finish_one()
+            finishing.extend([(interleave_y, (u, half)) for half in range(HALVES)])
+            finishing.extend([(quantize_y, (u, half)) for half in range(HALVES)])
 
-        def last_unit():
-            u = LAST
-            y[u] = work.tile([P, PACK, F], F32, name="y", bufs=6)
-            for half in range(HALVES):
-                scalar_slots = (0, 2, 1)[: int(LM[half]) % 5]
-                for t in range(PACK):
-                    project_and_exp(u, t, half)
-                    if t - 1 in scalar_slots:
-                        gate_on_scalar(u, t - 1, half)
-                    if t not in scalar_slots:
-                        gate_on_vector(u, t, half, half + 1)
-                    if half == 1 and t % 2 == 1 and (t == 3 or 1 not in scalar_slots):
-                        store_y(u, 0 if (t == 1 or 1 in scalar_slots) else 2, t + 1, 1, 2)
-                    run_pending()
-                    if t < POPS[u] - 4:
-                        run_pending()
-                if half == 0:
-                    store_y(u, 0, PACK, 0, 1)
-                    pending.extend([(interleave_y, (u, half)), (quantize_y, (u, half))])
-            for k in range(len(pending)):
-                run_pending()
-            interleave_y(u, 1, LS)
-            quantize_y(u, 1)
-
-        first_unit()
-        for u in range(1, LAST):
-            unit_by_slots(u)
-        last_unit()
+        y[LAST] = work.tile([P, HALVES, PACK, HALF], F32, name="y", bufs=Y_BUFS)
+        for half in range(HALVES):
+            for t in range(PACK):
+                project_and_exp(LAST, t, half)
+                if t > 0:
+                    gate_on_scalar(LAST, t - 1, half)
+                if t == PACK - 1:
+                    gate_on_vector(LAST, t, half, half + 1)
+                    store_y(LAST, 0, PACK, half, half + 1)
+                finish_one()
+            if half == 0:
+                finishing.extend([(interleave_y, (LAST, 0)), (quantize_y, (LAST, 0))])
+        interleave_y(LAST, 1, VECTOR_COLUMNS)
+        quantize_y(LAST, 1)
+        assert not finishing

from contextlib import ExitStack

import concourse.mybir as mybir
from concourse.masks import make_identity

H, L, D, F = 4, 1024, 512, 1024
FLOPS = 2 * H * L * D * F

F32 = mybir.dt.float32
BF16 = mybir.dt.bfloat16
I32 = mybir.dt.int32
U32 = mybir.dt.uint32
U8 = mybir.dt.uint8
FP8X4 = mybir.dt.float8_e4m3fn_x4
ACT = mybir.ActivationFunctionType
ALU = mybir.AluOpType

P = 128
PACK = 4
GROUP = P * PACK
GROUPS = L // GROUP
HALF = 512
HALVES = F // HALF
PAIR = 2
QUADRANTS = 4
RUN = 4
UNITS = [(g, h) for g in range(GROUPS) for h in range(H)]
LAST = len(UNITS) - 1

VECTOR_EVICTS_BEFORE = 3
DEFER_BEFORE = 4
SCALAR_GATES_FROM = 5
VECTOR_COLUMNS = 352

PROJ_BANKS = 6
Y_BUFS = 6


def tile_gated_positive_key_features_g2_kernel(tc, keys, omega, half_norm, key_gate, out_0, out_1, out_2):
    nc = tc.nc
    words_hbm = out_1.rearrange("g p m t -> g p (m t)").bitcast(I32)
    scales_hbm = out_2.bitcast(I32)

    with ExitStack() as ctx:
        keep = ctx.enter_context(tc.tile_pool(name="keep", bufs=1))
        work = ctx.enter_context(tc.tile_pool(name="work", bufs=2))
        proj_banks = ctx.enter_context(tc.psum_pool(name="proj_banks", bufs=PROJ_BANKS))
        turn_banks = ctx.enter_context(tc.psum_pool(name="turn_banks", bufs=2))
        ctx.enter_context(tc.manual_schedule())

        identity = keep.tile([P, P], F32, name="identity")
        make_identity(nc, identity[:])

        rows = H * GROUPS
        per_key = keep.tile([P, GROUP], BF16, name="per_key")
        nc.vector.memset(per_key[:], 0.0)

        omega_raw = {}
        keys_raw = {}

        def load_omega(half):
            omega_raw[half] = keep.tile([P, PACK, HALF], BF16, name="omega_raw%d" % half)
            columns = omega[:, half * HALF : (half + 1) * HALF]
            nc.sync.dma_start(out=omega_raw[half][:], in_=columns.rearrange("(p j) f -> p j f", j=PACK))

        def load_first_keys(t0):
            g, h = UNITS[0]
            raw = keep.tile([P, PAIR, D], BF16, name="first_keys_raw%d" % t0)
            unit_rows = keys[h, g * GROUP : (g + 1) * GROUP, :].rearrange("(p t) d -> p t d", t=PACK)
            nc.sync.dma_start(out=raw[:], in_=unit_rows[:, t0 : t0 + PAIR, :])
            for t in range(t0, t0 + PAIR):
                keys_raw[0, t] = raw[:, t - t0, :]

        def load_keys(u0, u1):
            g, h0 = UNITS[u0]
            raw = keep.tile([P, u1 - u0, PACK * D], BF16, name="keys_raw%d" % u0)
            heads = keys[h0 : h0 + u1 - u0, g * GROUP : (g + 1) * GROUP, :]
            nc.sync.dma_start(out=raw[:], in_=heads.rearrange("h (p t) d -> p h (t d)", t=PACK))
            for u in range(u0, u1):
                for t in range(PACK):
                    keys_raw[u, t] = raw[:, u - u0, t * D : (t + 1) * D]

        load_first_keys(0)
        load_omega(0)
        nc.sync.dma_start(out=per_key[0:rows, :], in_=half_norm.rearrange("h (g l) -> (h g) l", g=GROUPS))
        nc.sync.dma_start(out=per_key[rows : 2 * rows, :], in_=key_gate.rearrange("h (g l) -> (h g) l", g=GROUPS))
        load_first_keys(PAIR)
        load_omega(1)
        load_keys(1, 2)
        load_keys(2, H)
        load_keys(H, 2 * H)

        neg_norm = keep.tile([P, 2, 2 * rows], F32, name="neg_norm")
        gate = keep.tile([P, 2, 2 * rows], F32, name="gate")

        def turn_per_key():
            bank = proj_banks.tile([P, 2, P], F32, name="per_key_turned", tag="proj")
            words = per_key[:].bitcast(F32)
            for w in range(2):
                nc.tensor.transpose(bank[:, w, :], words[:, w : GROUP // 2 : 2], identity[:])
            values = bank[:].bitcast(BF16)
            nc.scalar.activation(neg_norm[:], values[:, :, 0 : 2 * rows], ACT.Copy, scale=-1.0)
            nc.scalar.copy(gate[:], values[:, :, 2 * rows : 4 * rows])

        def per_key_column(table, u, t):
            g, h = UNITS[u]
            column = 2 * (h * GROUPS + g) + t % 2
            return table[:, t // 2, column : column + 1]

        def interleave(copy, dst, src):
            copy(
                out=dst.rearrange("p (c i) t -> p c t i", i=RUN),
                in_=src.rearrange("p t (c i) -> p c t i", i=RUN),
            )

        omega_grouped = {}
        omega_codes = {}
        omega_scales = {}

        def interleave_omega(half):
            omega_grouped[half] = keep.tile([P, HALF, PACK], BF16, name="omega_grouped%d" % half, align_bytes=64)
            interleave(nc.vector.tensor_copy, omega_grouped[half][:], omega_raw[half][:])

        def quantize_omega(half):
            omega_codes[half] = keep.tile([P, HALF], U32, name="omega_codes%d" % half, align_bytes=64)
            omega_scales[half] = keep.tile([P, HALF], U8, name="omega_scales%d" % half, align_bytes=64)
            nc.vector.quantize_mx(
                out=omega_codes[half][:].bitcast(FP8X4),
                scales=omega_scales[half][:],
                in_=omega_grouped[half][:].rearrange("p f j -> p (f j)"),
            )

        keys_turned = {}
        keys_grouped = {}
        keys_grouped_pair = {}
        key_codes = {}
        key_scales = {}

        def turn_keys(u, t0):
            keys_turned[u, t0] = turn_banks.tile([P, PAIR, 2, P], F32, name="keys_turned")
            for t in range(t0, t0 + PAIR):
                words = keys_raw[u, t].bitcast(F32)
                for w in range(2):
                    nc.tensor.transpose(keys_turned[u, t0][:, t - t0, w, :], words[:, w : D // 2 : 2], identity[:])

        def new_keys_grouped(u, t0, t1):
            grouped = work.tile([P, (t1 - t0) * P * PACK], BF16, name="keys_grouped", bufs=3, align_bytes=64)
            keys_grouped[u, t0] = grouped
            for t in range(t0, t1, PAIR):
                keys_grouped_pair[u, t] = grouped[:, (t - t0) * P * PACK : (t - t0 + PAIR) * P * PACK]

        def evict_keys(u, t0, copy):
            copy(
                out=keys_grouped_pair[u, t0].bitcast(F32).rearrange("p (s m w) -> p s m w", s=PAIR, w=2),
                in_=keys_turned[u, t0][:].rearrange("p s w m -> p s m w"),
            )

        def quantize_keys(u, t0, t1):
            if t0 == 0:
                key_codes[u] = work.tile([P, PACK * P], U32, name="key_codes", bufs=3, align_bytes=64)
                key_scales[u] = work.tile([P, PACK * P], U8, name="key_scales", bufs=3, align_bytes=64)
            columns = slice(t0 * P, t1 * P)
            nc.vector.quantize_mx(
                out=key_codes[u][:, columns].bitcast(FP8X4),
                scales=key_scales[u][:, columns],
                in_=keys_grouped[u, t0][:],
            )

        def turn_unit_keys(u):
            for t0 in range(0, PACK, PAIR):
                turn_keys(u, t0)
            new_keys_grouped(u, 0, PACK)

        y = {}
        y_grouped = {}
        y_words = {}
        y_scales = {}

        def y_part(u, t0, t1, f0, f1):
            if u in (0, LAST):
                half = f0 // HALF
                return y[u][:, half, t0:t1, f0 - half * HALF : f1 - half * HALF]
            return y[u][:, t0:t1, f0:f1]

        def y_slot(u, t, half0, half1):
            return y_part(u, t, t + 1, half0 * HALF, half1 * HALF)[:, 0, :]

        def project_and_exp(u, t, half):
            bank = proj_banks.tile([P, HALF], F32, name="proj", tag="proj")
            columns = slice(t * P, (t + 1) * P)
            nc.tensor.matmul_mx(
                out=bank[:],
                lhsT=key_codes[u][:, columns].bitcast(FP8X4),
                lhsT_scale=key_scales[u][:, columns],
                rhs=omega_codes[half][:].bitcast(FP8X4),
                rhs_scale=omega_scales[half][:],
                start=True,
                stop=True,
            )
            nc.scalar.activation(y_slot(u, t, half, half + 1), bank[:], ACT.Exp, bias=per_key_column(neg_norm, u, t))

        def gate_on_vector(u, t, half0, half1):
            part = y_slot(u, t, half0, half1)
            nc.vector.tensor_scalar(part, part, per_key_column(gate, u, t), None, ALU.mult)

        def gate_on_scalar(u, t, half):
            part = y_slot(u, t, half, half + 1)
            nc.scalar.activation(part, part, ACT.Copy, scale=per_key_column(gate, u, t))

        def store_y(u, t0, t1, half0, half1):
            g, h = UNITS[u]
            unit_rows = out_0[h, g * GROUP : (g + 1) * GROUP, :].rearrange("(p t) f -> p t f", t=PACK)
            f0, f1 = half0 * HALF, half1 * HALF
            nc.sync.dma_start(out=unit_rows[:, t0:t1, f0:f1], in_=y_part(u, t0, t1, f0, f1))

        def interleave_y(u, half, vector_columns=HALF):
            grouped = work.tile([P, HALF, PACK], BF16, name="y_grouped", bufs=4, align_bytes=64)
            y_grouped[u, half] = grouped
            f0 = half * HALF
            cut = f0 + vector_columns
            interleave(nc.vector.tensor_copy, grouped[:, 0:vector_columns, :], y_part(u, 0, PACK, f0, cut))
            if vector_columns < HALF:
                interleave(nc.scalar.copy, grouped[:, vector_columns:HALF, :], y_part(u, 0, PACK, cut, f0 + HALF))

        def quantize_y(u, half):
            g, h = UNITS[u]
            if h == 0 and half == 0:
                y_words[g] = work.tile([P, H * F], U32, name="y_words", align_bytes=64)
                y_scales[g] = work.tile([P, F], U8, name="y_scales", align_bytes=64)
            m0 = h * F + half * HALF
            nc.vector.quantize_mx(
                out=y_words[g][:, m0 : m0 + HALF].bitcast(FP8X4),
                scales=y_scales[g][4 * h : P, half * HALF : (half + 1) * HALF],
                in_=y_grouped[u, half][:].rearrange("p f t -> p (f t)"),
            )
            if u == LAST or half == HALVES - 1:
                columns = slice(m0 if u == LAST else h * F, m0 + HALF)
                nc.sync.dma_start(out=words_hbm[g, :, columns], in_=y_words[g][:, columns].bitcast(I32))
            if h == H - 1 and half == HALVES - 1:
                for q in range(QUADRANTS):
                    blocks = scales_hbm[g, 4 * q : 4 * q + 4, :].rearrange("r (h m) -> h r m", h=H)
                    nc.sync.dma_start(out=blocks, in_=y_scales[g][32 * q : 32 * q + 4 * H, :].bitcast(I32))

        finishing = []

        def finish_one():
            if finishing:
                step = finishing[0]
                finishing.remove(step)
                step[0](*step[1])

        new_keys_grouped(0, 0, PAIR)
        new_keys_grouped(0, PAIR, PACK)
        interleave_omega(0)
        turn_keys(0, 0)
        evict_keys(0, 0, nc.scalar.copy)
        turn_per_key()
        quantize_keys(0, 0, PAIR)
        quantize_omega(0)
        interleave_omega(1)
        turn_keys(0, PAIR)
        evict_keys(0, PAIR, nc.scalar.copy)
        quantize_keys(0, PAIR, PACK)
        quantize_omega(1)

        y[0] = work.tile([P, HALVES, PACK, HALF], F32, name="y", bufs=Y_BUFS)
        for t in range(PACK):
            project_and_exp(0, t, 0)
            gate_on_vector(0, t, 0, 1)
        store_y(0, 0, PACK, 0, 1)
        turn_unit_keys(1)
        evict_keys(1, 0, nc.scalar.copy)
        evict_keys(1, PAIR, nc.scalar.copy)
        interleave_y(0, 0)
        for t in range(PACK):
            project_and_exp(0, t, 1)
            gate_on_vector(0, t, 1, 2)
            if t == 0:
                quantize_keys(1, 0, PACK)
            if t == 1:
                quantize_y(0, 0)
        store_y(0, 0, PACK, 1, 2)
        finishing.extend([(interleave_y, (0, 1)), (quantize_y, (0, 1))])

        for u in range(1, LAST):
            y[u] = work.tile([P, PACK, F], F32, name="y", bufs=Y_BUFS)
            turn_unit_keys(u + 1)
            for t in range(PACK):
                project_and_exp(u, t, 0)
                project_and_exp(u, t, 1)
                if t == 0:
                    evict_keys(u + 1, 0, nc.vector.tensor_copy if u < VECTOR_EVICTS_BEFORE else nc.scalar.copy)
                if t == 1:
                    evict_keys(u + 1, PAIR, nc.scalar.copy)
                if u >= SCALAR_GATES_FROM and t >= PAIR:
                    gate_on_scalar(u, t, 0)
                    gate_on_vector(u, t, 1, 2)
                else:
                    gate_on_vector(u, t, 0, 2)
                if t % PAIR == PAIR - 1:
                    store_y(u, t + 1 - PAIR, t + 1, 0, 2)
                if t == 1:
                    quantize_keys(u + 1, 0, PACK)
                if u >= DEFER_BEFORE or t < PACK - 1:
                    finish_one()
            finishing.extend([(interleave_y, (u, half)) for half in range(HALVES)])
            finishing.extend([(quantize_y, (u, half)) for half in range(HALVES)])

        y[LAST] = work.tile([P, HALVES, PACK, HALF], F32, name="y", bufs=Y_BUFS)
        for half in range(HALVES):
            for t in range(PACK):
                project_and_exp(LAST, t, half)
                if t > 0:
                    gate_on_scalar(LAST, t - 1, half)
                if t == PACK - 1:
                    gate_on_vector(LAST, t, half, half + 1)
                    store_y(LAST, 0, PACK, half, half + 1)
                finish_one()
            if half == 0:
                finishing.extend([(interleave_y, (LAST, 0)), (quantize_y, (LAST, 0))])
        interleave_y(LAST, 1, VECTOR_COLUMNS)
        quantize_y(LAST, 1)
        assert not finishing
